import numpy as np
import ml_dtypes


def mxq(x, axis, fmt="e4m3"):
    dtype, down = {"e4m3": (ml_dtypes.float8_e4m3fn, 7), "e5m2": (ml_dtypes.float8_e5m2, 14)}[fmt]
    v = np.moveaxis(np.asarray(x, np.float32).astype(ml_dtypes.bfloat16).astype(np.float64), axis, -1)
    blocks = v.reshape(v.shape[:-1] + (-1, 32))
    amax = np.abs(blocks).max(-1, keepdims=True)
    byte = np.maximum(np.where(amax > 0, np.frexp(amax)[1] - 1 + 127, 0) - down, 1)
    scale = np.exp2(byte - 127.0)
    codes = (blocks / scale).astype(np.float32).astype(dtype).astype(np.float64)
    return np.moveaxis((codes * scale).reshape(v.shape), -1, axis)


WIDE = False


def mx_kscale(k):
    if not WIDE:
        return np.ones(k)
    levels = np.array([10, -10, 5, -5, 0])
    if k % 512:
        return np.exp2(np.random.permutation(np.resize(levels, k // 32))).repeat(32)
    a = np.empty((k // 512, 16))
    for p in range(k // 512):
        a[p, :8] = np.random.permutation(np.resize(levels, 8))
        for g in range(8):
            far = levels[np.abs(levels - a[p, g]) >= 10]
            a[p, g + 8] = far[np.random.randint(len(far))]
    return np.exp2(a.ravel()).repeat(32)


def f64(x):
    return np.asarray(x).astype(np.float64)


def striped8(idx):
    return np.concatenate([v.reshape(-1, 16).T for v in idx]).astype(np.uint16)


def unstriped8(offs):
    return np.stack([offs[16 * g:16 * g + 16].T.reshape(-1) for g in range(8)]).astype(np.int64)


E2M1 = np.array([0.0, 0.5, 1.0, 1.5, 2.0, 3.0, 4.0, 6.0, -0.0, -0.5, -1.0, -1.5, -2.0, -3.0, -4.0, -6.0])


def pack_weight(w, fmt):
    k, n = w.shape
    w = f64(np.asarray(w, np.float32).astype(ml_dtypes.bfloat16)).reshape(k // 32, 32, n)
    amax = np.abs(w).max(1)
    if fmt == "e4m3":
        byte = np.frexp(amax)[1] - 1 + 127 - 7
    else:
        mant, ex = np.frexp(amax / 6.0)
        byte = np.where(mant > 0.5, ex, ex - 1) + 127
    byte = np.clip(np.where(amax > 0, byte, 1), 1, 254)
    scaled = (w * np.exp2(127.0 - byte)[:, None, :]).reshape(k, n).astype(np.float32)
    by_word = np.ascontiguousarray(scaled.reshape(k // 512, 128, 4, n).transpose(0, 1, 3, 2))
    if fmt == "e4m3":
        words = by_word.astype(ml_dtypes.float8_e4m3fn).view(np.uint8)
    else:
        c = by_word.astype(ml_dtypes.float4_e2m1fn).view(np.uint8) & 0xF
        words = (c[..., 0::2] | (c[..., 1::2] << 4)).reshape(k // 512, 128, 2 * n)
    return np.ascontiguousarray(words), np.ascontiguousarray(byte.astype(np.uint8).reshape(k // 512, 16, n))


def unpack_weight(words, scales, fmt):
    g, _, n = scales.shape
    words = np.ascontiguousarray(words).reshape(g, 128, n, -1)
    if fmt == "e4m3":
        vals = words.view(ml_dtypes.float8_e4m3fn).astype(np.float64)
    else:
        nib = np.empty((g, 128, n, 4), np.uint8)
        nib[..., 0::2] = words & 0xF
        nib[..., 1::2] = words >> 4
        vals = E2M1[nib]
    vals = vals * np.repeat(np.exp2(scales.astype(np.float64) - 127.0), 8, axis=1)[..., None]
    return vals.transpose(0, 1, 3, 2).reshape(g * 512, n)


K, M, T, S = 512, 128, 1024, 512


def setup_inputs():
    n = np.random.standard_normal
    s = mx_kscale(K)[:, None]
    u = mx_kscale(512)[:, None]
    p_w2 = pack_weight(1.4 * n((512, M)) / np.sqrt(512) / u, "e2m1")
    return {
        "xT": (n((K, T)) * s).astype(np.float32),
        "w1": (n((K, 512)) / np.sqrt(K) / s * u.T).astype(np.float32),
        "w2_words": p_w2[0],
        "w2_scales": p_w2[1],
        "wgt": np.repeat(np.random.uniform(0.5, 2.0, (8, S)), 16, axis=0).astype(np.float32),
        "wgo": np.repeat(np.random.uniform(0.5, 2.0, (8, S)), 16, axis=0).astype(np.float32),
        "offs": striped8(np.stack([np.random.permutation(T)[:S] for _ in range(8)])),
        "offs2": striped8(np.stack([np.random.permutation(T)[:S] for _ in range(8)])),
    }


def reference(xT, w1, w2_words, w2_scales, wgt, wgo, offs, offs2):
    idx = unstriped8(offs)
    group = np.arange(K) % 512 // 64
    xg = f64(wgt)[np.arange(K) // 4 % 128] * f64(xT)[np.arange(K)[:, None], idx[group]]
    xT_ = mxq(xg, 0, "e4m3")
    w1_ = mxq(f64(w1), 0, "e4m3")
    w2_ = unpack_weight(w2_words, w2_scales, "e2m1")
    h_ = mxq(np.maximum(w1_.T @ xT_, 0.0), 0, "e4m3")
    y = w2_.T @ h_
    place = unstriped8(offs2)[np.arange(M) % 128 // 16]
    out = np.zeros((M, T))
    out[np.arange(M)[:, None], place] = f64(wgo)[np.arange(M) % 128] * (y)
    return out

@@ -1,0 +1,154 @@
+from contextlib import ExitStack
+
+import concourse.mybir as mybir
+
+K, H, M, T, S = 512, 512, 128, 1024, 512
+FLOPS = 2 * K * H * S + 2 * H * M * S
+
+F32 = mybir.dt.float32
+BF16 = mybir.dt.bfloat16
+I32 = mybir.dt.int32
+U32 = mybir.dt.uint32
+U16 = mybir.dt.uint16
+U8 = mybir.dt.uint8
+FP8X4 = mybir.dt.float8_e4m3fn_x4
+FP4X4 = mybir.dt.float4_e2m1fn_x4
+MULT = mybir.AluOpType.mult
+MAX = mybir.AluOpType.max
+RELU = mybir.ActivationFunctionType.Relu
+
+P = 128
+PACK = 4
+CH = 128
+NCH = S // CH
+LC = CH // 16
+HALF = H // 2
+
+
+def tile_list_hboth_m_none_kernel(tc, xT, w1, w2_words, w2_scales, wgt, wgo, offs, offs2, out):
+    nc = tc.nc
+    with ExitStack() as ctx:
+        sb = ctx.enter_context(tc.tile_pool(name="sb", bufs=1))
+        ps = ctx.enter_context(tc.psum_pool(name="ps", bufs=1))
+
+        idx = sb.tile([P, S // 16], U16, name="idx")
+        idx2 = sb.tile([P, S // 16], U16, name="idx2")
+        w_raw = [sb.tile([P, PACK, HALF], F32, name="w_raw%d" % a) for a in range(2)]
+        planes = [sb.tile([P, T], F32, name="plane%d" % i) for i in range(PACK)]
+        wgt_sb = sb.tile([P, S], F32, name="wgt_sb")
+        wgo_sb = sb.tile([P, S], F32, name="wgo_sb")
+        w2_codes = sb.tile([P, 2 * M], U8, name="w2_codes", align_bytes=64)
+        w2_sc = sb.tile([P, M], U8, name="w2_sc", align_bytes=64)
+        page = sb.tile([P, T], F32, name="page")
+
+        w1_rows = w1.rearrange("(p j) c -> p j c", j=PACK)
+        x_rows = xT.rearrange("(p i) t -> p i t", i=PACK)
+
+        nc.sync.dma_start(out=w_raw[0][:], in_=w1_rows[:, :, 0:HALF])
+        nc.sync.dma_start(idx[:], offs)
+        nc.sync.dma_start(out=w_raw[1][:], in_=w1_rows[:, :, HALF:H])
+        nc.sync.dma_start(out=wgt_sb[:], in_=wgt)
+        for i in range(PACK):
+            nc.sync.dma_start(out=planes[i][:], in_=x_rows[:, i, :])
+        nc.sync.dma_start(out=wgo_sb[:], in_=wgo)
+        nc.sync.dma_start(idx2[:], offs2)
+        nc.sync.dma_start(out=w2_codes[:].bitcast(I32), in_=w2_words[0].bitcast(I32))
+        nc.vector.memset(w2_sc[:].bitcast(I32), 0)
+        for q in range(4):
+            nc.sync.dma_start(out=w2_sc[32 * q : 32 * q + 4, :].bitcast(I32),
+                                in_=w2_scales[0, 4 * q : 4 * q + 4, :].bitcast(I32))
+        nc.vector.memset(page[:], 0.0)
+
+        w_bf = sb.tile([P, H * PACK], BF16, name="w_bf", align_bytes=64)
+        w_view = w_bf[:].rearrange("p (t m j) -> p m j t", t=PACK, j=PACK)
+        mh = HALF // PACK
+        nc.scalar.copy(out=w_view[:, 0:mh], in_=w_raw[0][:].rearrange("p j (m t) -> p m j t", t=PACK))
+        nc.vector.tensor_copy(out=w_view[:, mh : 2 * mh], in_=w_raw[1][:].rearrange("p j (m t) -> p m j t", t=PACK))
+        w1_codes = sb.tile([P, H], U32, name="w1_codes", align_bytes=64)
+        w1_sc = sb.tile([P, H], U8, name="w1_sc", align_bytes=64)
+        nc.vector.quantize_mx(out=w1_codes[:].bitcast(FP8X4), scales=w1_sc[:], in_=w_bf[:])
+
+        picked = sb.tile([P, PACK, S], F32, name="picked")
+        for i in range(PACK - 1):
+            nc.vector.tensor_tensor(picked[:, i, :], planes[i][:].indirect(idx[:]), wgt_sb[:], MULT)
+        for c in range(NCH):
+            cols = slice(c * CH, (c + 1) * CH)
+            nc.vector.tensor_tensor(picked[:, PACK - 1, cols],
+                                    planes[PACK - 1][:].indirect(idx[:, c * LC : (c + 1) * LC]),
+                                    wgt_sb[:, cols], MULT)
+
+        x_bf, x_codes, x_sc, h_ps, h_bf, h_codes, h_sc, y_ps = [], [], [], [], [], [], [], []
+        for c in range(NCH):
+            x_bf.append(sb.tile([P, CH * PACK], BF16, name="x_bf%d" % c, align_bytes=64))
+            x_codes.append(sb.tile([P, CH], U32, name="x_codes%d" % c, align_bytes=64))
+            x_sc.append(sb.tile([P, CH], U8, name="x_sc%d" % c, align_bytes=64))
+            h_bf.append(sb.tile([P, CH * PACK], BF16, name="h_bf%d" % c, align_bytes=64))
+            h_codes.append(sb.tile([P, CH], U32, name="h_codes%d" % c, align_bytes=64))
+            h_sc.append(sb.tile([P, CH], U8, name="h_sc%d" % c, align_bytes=64))
+            h_ps.append(ps.tile([P, PACK, CH], F32, name="h_ps%d" % c))
+            y_ps.append(ps.tile([P, CH], F32, name="y_ps%d" % c))
+        y_tiles = [sb.tile([P, CH], F32, name="y_a"), sb.tile([P, CH], F32, name="y_b"), sb.tile([P, 2 * CH], F32, name="y_c")]
+        y_sb = [y_tiles[0][:], y_tiles[1][:], y_tiles[2][:, 0:CH], y_tiles[2][:, CH : 2 * CH]]
+
+        def weave(c, on_vector):
+            dst = x_bf[c][:].rearrange("p (a s i) -> p a i s", s=4, i=PACK)
+            src = picked[:, :, c * CH : (c + 1) * CH].rearrange("p i (a s) -> p a i s", s=4)
+            if on_vector:
+                nc.vector.tensor_copy(out=dst, in_=src)
+            else:
+                nc.scalar.copy(out=dst, in_=src)
+
+        def first(c):
+            nc.vector.quantize_mx(out=x_codes[c][:].bitcast(FP8X4), scales=x_sc[c][:], in_=x_bf[c][:])
+            for t in range(PACK):
+                nc.tensor.matmul_mx(out=h_ps[c][:, t, :],
+                                    lhsT=w1_codes[:, t * P : (t + 1) * P].bitcast(FP8X4),
+                                    lhsT_scale=w1_sc[:, t * P : (t + 1) * P],
+                                    rhs=x_codes[c][:].bitcast(FP8X4), rhs_scale=x_sc[c][:],
+                                    start=True, stop=True)
+
+        def relu(c, on_vector):
+            dst = h_bf[c][:].rearrange("p (s t) -> p s t", t=PACK)
+            src = h_ps[c][:].rearrange("p t s -> p s t")
+            if on_vector:
+                nc.vector.tensor_scalar(dst, src, 0.0, None, MAX)
+            else:
+                nc.scalar.activation(dst, src, RELU)
+
+        def second(c):
+            nc.vector.quantize_mx(out=h_codes[c][:].bitcast(FP8X4), scales=h_sc[c][:], in_=h_bf[c][:])
+            nc.tensor.matmul_mx(out=y_ps[c][:], lhsT=w2_codes[:].bitcast(FP4X4), lhsT_scale=w2_sc[:],
+                                rhs=h_codes[c][:].bitcast(FP8X4), rhs_scale=h_sc[c][:],
+                                start=True, stop=True)
+
+        def leave(c):
+            nc.scalar.copy(out=y_sb[c], in_=y_ps[c][:])
+
+        def place(c0, c1):
+            cols = slice(c0 * CH, c1 * CH)
+            nc.vector.tensor_tensor(page[:].indirect(idx2[:, c0 * LC : c1 * LC]), y_tiles[c0][:], wgo_sb[:, cols], MULT)
+
+        weave(0, False)
+        weave(1, False)
+        first(0)
+        weave(2, True)
+        first(1)
+        weave(3, True)
+        relu(0, False)
+        first(2)
+        first(3)
+        relu(1, False)
+        second(0)
+        relu(2, False)
+        leave(0)
+        second(1)
+        relu(3, False)
+        place(0, 1)
+        leave(1)
+        second(2)
+        second(3)
+        place(1, 2)
+        leave(2)
+        leave(3)
+        place(2, 4)
+        nc.sync.dma_start(out=out, in_=page[:])

@@ -44,38 +44,49 @@ def tile_list_hboth_m_none_kernel(tc, xT, w1, w2_words, w2_scales, wgt, wgo, off
         w1_rows = w1.rearrange("(p j) c -> p j c", j=PACK)
         x_rows = xT.rearrange("(p i) t -> p i t", i=PACK)
 
-        nc.sync.dma_start(out=w_raw[0][:], in_=w1_rows[:, :, 0:HALF])
-        nc.sync.dma_start(idx[:], offs)
-        nc.sync.dma_start(out=w_raw[1][:], in_=w1_rows[:, :, HALF:H])
-        nc.sync.dma_start(out=wgt_sb[:], in_=wgt)
-        for i in range(PACK):
-            nc.sync.dma_start(out=planes[i][:], in_=x_rows[:, i, :])
-        nc.sync.dma_start(out=wgo_sb[:], in_=wgo)
-        nc.sync.dma_start(idx2[:], offs2)
-        nc.sync.dma_start(out=w2_codes[:].bitcast(I32), in_=w2_words[0].bitcast(I32))
-        nc.vector.memset(w2_sc[:].bitcast(I32), 0)
+        nc.gpsimd.dma_start(out=w2_codes[:].bitcast(I32), in_=w2_words[0].bitcast(I32))
+        nc.gpsimd.memset(w2_sc[:].bitcast(I32), 0)
         for q in range(4):
-            nc.sync.dma_start(out=w2_sc[32 * q : 32 * q + 4, :].bitcast(I32),
+            nc.gpsimd.dma_start(out=w2_sc[32 * q : 32 * q + 4, :].bitcast(I32),
                                 in_=w2_scales[0, 4 * q : 4 * q + 4, :].bitcast(I32))
+        nc.sync.dma_start(out=w_raw[0][:], in_=w1_rows[:, :, 0:HALF])
+        nc.sync.dma_start(out=planes[0][:], in_=x_rows[:, 0, :])
+        nc.sync.dma_start(idx[:], offs)
+        nc.sync.dma_start(out=wgt_sb[:], in_=wgt)
+        nc.sync.dma_start(out=w_raw[1][:], in_=w1_rows[:, :, HALF:H])
+        for i in range(1, PACK):
+            nc.sync.dma_start(out=planes[i][:], in_=x_rows[:, i, :])
+        nc.sync.dma_start(idx2[:], offs2)
+        nc.sync.dma_start(out=wgo_sb[:], in_=wgo)
         nc.vector.memset(page[:], 0.0)
 
         w_bf = sb.tile([P, H * PACK], BF16, name="w_bf", align_bytes=64)
         w_view = w_bf[:].rearrange("p (t m j) -> p m j t", t=PACK, j=PACK)
         mh = HALF // PACK
-        nc.scalar.copy(out=w_view[:, 0:mh], in_=w_raw[0][:].rearrange("p j (m t) -> p m j t", t=PACK))
-        nc.vector.tensor_copy(out=w_view[:, mh : 2 * mh], in_=w_raw[1][:].rearrange("p j (m t) -> p m j t", t=PACK))
         w1_codes = sb.tile([P, H], U32, name="w1_codes", align_bytes=64)
         w1_sc = sb.tile([P, H], U8, name="w1_sc", align_bytes=64)
-        nc.vector.quantize_mx(out=w1_codes[:].bitcast(FP8X4), scales=w1_sc[:], in_=w_bf[:])
-
         picked = sb.tile([P, PACK, S], F32, name="picked")
-        for i in range(PACK - 1):
-            nc.vector.tensor_tensor(picked[:, i, :], planes[i][:].indirect(idx[:]), wgt_sb[:], MULT)
-        for c in range(NCH):
-            cols = slice(c * CH, (c + 1) * CH)
-            nc.vector.tensor_tensor(picked[:, PACK - 1, cols],
-                                    planes[PACK - 1][:].indirect(idx[:, c * LC : (c + 1) * LC]),
+
+        def weights(a, on_scalar):
+            src = w_raw[a][:].rearrange("p j (m t) -> p m j t", t=PACK)
+            nc.scalar.copy(out=w_view[:, a * mh : a * mh + on_scalar], in_=src[:, 0:on_scalar])
+            if on_scalar < mh:
+                nc.vector.tensor_copy(out=w_view[:, a * mh + on_scalar : (a + 1) * mh], in_=src[:, on_scalar:mh])
+            for t in range(PACK):
+                c0 = t * P + a * mh
+                nc.vector.quantize_mx(out=w1_codes[:, c0 : c0 + mh].bitcast(FP8X4), scales=w1_sc[:, c0 : c0 + mh],
+                                      in_=w_bf[:, c0 * PACK : (c0 + mh) * PACK])
+
+        def pick(i, c0, c1):
+            cols = slice(c0 * CH, c1 * CH)
+            nc.vector.tensor_tensor(picked[:, i, cols], planes[i][:].indirect(idx[:, c0 * LC : c1 * LC]),
                                     wgt_sb[:, cols], MULT)
+
+        weights(0, mh)
+        pick(0, 0, NCH)
+        weights(1, 24)
+        pick(1, 0, NCH)
+        pick(2, 0, NCH)
 
         x_bf, x_codes, x_sc, h_ps, h_bf, h_codes, h_sc, y_ps = [], [], [], [], [], [], [], []
         for c in range(NCH):
@@ -122,33 +133,23 @@ def tile_list_hboth_m_none_kernel(tc, xT, w1, w2_words, w2_scales, wgt, wgo, off
                                 start=True, stop=True)
 
         def leave(c):
-            nc.scalar.copy(out=y_sb[c], in_=y_ps[c][:])
+            if c == 0:
+                nc.vector.tensor_copy(out=y_sb[c], in_=y_ps[c][:])
+            else:
+                nc.scalar.copy(out=y_sb[c], in_=y_ps[c][:])
 
         def place(c0, c1):
             cols = slice(c0 * CH, c1 * CH)
             nc.vector.tensor_tensor(page[:].indirect(idx2[:, c0 * LC : c1 * LC]), y_tiles[c0][:], wgo_sb[:, cols], MULT)
 
-        weave(0, False)
-        weave(1, False)
-        first(0)
-        weave(2, True)
-        first(1)
-        weave(3, True)
-        relu(0, False)
-        first(2)
-        first(3)
-        relu(1, False)
-        second(0)
-        relu(2, False)
-        leave(0)
-        second(1)
-        relu(3, False)
-        place(0, 1)
-        leave(1)
-        second(2)
-        second(3)
-        place(1, 2)
-        leave(2)
-        leave(3)
-        place(2, 4)
+        for c in range(NCH):
+            pick(PACK - 1, c, c + 1)
+            weave(c, c >= 2)
+            first(c)
+            relu(c, False)
+            second(c)
+            leave(c)
+            if c < 2:
+                place(c, c + 1)
+        place(2, NCH)
         nc.sync.dma_start(out=out, in_=page[:])

@@ -22,7 +22,7 @@ PACK = 4
 CH = 128
 NCH = S // CH
 LC = CH // 16
-HALF = H // 2
+W_SCALAR = 72
 
 
 def tile_list_hboth_m_none_kernel(tc, xT, w1, w2_words, w2_scales, wgt, wgo, offs, offs2, out):
@@ -33,7 +33,7 @@ def tile_list_hboth_m_none_kernel(tc, xT, w1, w2_words, w2_scales, wgt, wgo, off
 
         idx = sb.tile([P, S // 16], U16, name="idx")
         idx2 = sb.tile([P, S // 16], U16, name="idx2")
-        w_raw = [sb.tile([P, PACK, HALF], F32, name="w_raw%d" % a) for a in range(2)]
+        w_raw = sb.tile([P, PACK, H], F32, name="w_raw")
         planes = [sb.tile([P, T], F32, name="plane%d" % i) for i in range(PACK)]
         wgt_sb = sb.tile([P, S], F32, name="wgt_sb")
         wgo_sb = sb.tile([P, S], F32, name="wgo_sb")
@@ -49,44 +49,36 @@ def tile_list_hboth_m_none_kernel(tc, xT, w1, w2_words, w2_scales, wgt, wgo, off
         for q in range(4):
             nc.gpsimd.dma_start(out=w2_sc[32 * q : 32 * q + 4, :].bitcast(I32),
                                 in_=w2_scales[0, 4 * q : 4 * q + 4, :].bitcast(I32))
-        nc.sync.dma_start(out=w_raw[0][:], in_=w1_rows[:, :, 0:HALF])
         nc.sync.dma_start(out=planes[0][:], in_=x_rows[:, 0, :])
         nc.sync.dma_start(idx[:], offs)
         nc.sync.dma_start(out=wgt_sb[:], in_=wgt)
-        nc.sync.dma_start(out=w_raw[1][:], in_=w1_rows[:, :, HALF:H])
-        for i in range(1, PACK):
-            nc.sync.dma_start(out=planes[i][:], in_=x_rows[:, i, :])
+        nc.sync.dma_start(out=planes[1][:], in_=x_rows[:, 1, :])
+        nc.sync.dma_start(out=planes[2][:], in_=x_rows[:, 2, :])
+        nc.sync.dma_start(out=w_raw[:, 0:2, :], in_=w1_rows[:, 0:2, :])
+        nc.sync.dma_start(out=w_raw[:, 2:4, :], in_=w1_rows[:, 2:4, :])
+        nc.sync.dma_start(out=planes[3][:], in_=x_rows[:, 3, :])
         nc.sync.dma_start(idx2[:], offs2)
         nc.sync.dma_start(out=wgo_sb[:], in_=wgo)
         nc.vector.memset(page[:], 0.0)
+        zero = sb.tile([P, 1], F32, name="zero")
+        nc.scalar.copy(out=zero[:], in_=page[:, 0:1])
 
         w_bf = sb.tile([P, H * PACK], BF16, name="w_bf", align_bytes=64)
         w_view = w_bf[:].rearrange("p (t m j) -> p m j t", t=PACK, j=PACK)
-        mh = HALF // PACK
         w1_codes = sb.tile([P, H], U32, name="w1_codes", align_bytes=64)
         w1_sc = sb.tile([P, H], U8, name="w1_sc", align_bytes=64)
         picked = sb.tile([P, PACK, S], F32, name="picked")
-
-        def weights(a, on_scalar):
-            src = w_raw[a][:].rearrange("p j (m t) -> p m j t", t=PACK)
-            nc.scalar.copy(out=w_view[:, a * mh : a * mh + on_scalar], in_=src[:, 0:on_scalar])
-            if on_scalar < mh:
-                nc.vector.tensor_copy(out=w_view[:, a * mh + on_scalar : (a + 1) * mh], in_=src[:, on_scalar:mh])
-            for t in range(PACK):
-                c0 = t * P + a * mh
-                nc.vector.quantize_mx(out=w1_codes[:, c0 : c0 + mh].bitcast(FP8X4), scales=w1_sc[:, c0 : c0 + mh],
-                                      in_=w_bf[:, c0 * PACK : (c0 + mh) * PACK])
 
         def pick(i, c0, c1):
             cols = slice(c0 * CH, c1 * CH)
             nc.vector.tensor_tensor(picked[:, i, cols], planes[i][:].indirect(idx[:, c0 * LC : c1 * LC]),
                                     wgt_sb[:, cols], MULT)
 
-        weights(0, mh)
-        pick(0, 0, NCH)
-        weights(1, 24)
-        pick(1, 0, NCH)
-        pick(2, 0, NCH)
+        for i in range(PACK - 1):
+            pick(i, 0, NCH)
+        w_src = w_raw[:].rearrange("p j (m t) -> p m j t", t=PACK)
+        nc.scalar.copy(out=w_view[:, 0:W_SCALAR], in_=w_src[:, 0:W_SCALAR])
+        nc.vector.tensor_copy(out=w_view[:, W_SCALAR:P], in_=w_src[:, W_SCALAR:P])
 
         x_bf, x_codes, x_sc, h_ps, h_bf, h_codes, h_sc, y_ps = [], [], [], [], [], [], [], []
         for c in range(NCH):
@@ -98,8 +90,7 @@ def tile_list_hboth_m_none_kernel(tc, xT, w1, w2_words, w2_scales, wgt, wgo, off
             h_sc.append(sb.tile([P, CH], U8, name="h_sc%d" % c, align_bytes=64))
             h_ps.append(ps.tile([P, PACK, CH], F32, name="h_ps%d" % c))
             y_ps.append(ps.tile([P, CH], F32, name="y_ps%d" % c))
-        y_tiles = [sb.tile([P, CH], F32, name="y_a"), sb.tile([P, CH], F32, name="y_b"), sb.tile([P, 2 * CH], F32, name="y_c")]
-        y_sb = [y_tiles[0][:], y_tiles[1][:], y_tiles[2][:, 0:CH], y_tiles[2][:, CH : 2 * CH]]
+        y_sb = [sb.tile([P, CH], F32, name="y_sb%d" % c) for c in range(NCH)]
 
         def weave(c, on_vector):
             dst = x_bf[c][:].rearrange("p (a s i) -> p a i s", s=4, i=PACK)
@@ -124,7 +115,7 @@ def tile_list_hboth_m_none_kernel(tc, xT, w1, w2_words, w2_scales, wgt, wgo, off
             if on_vector:
                 nc.vector.tensor_scalar(dst, src, 0.0, None, MAX)
             else:
-                nc.scalar.activation(dst, src, RELU)
+                nc.scalar.activation(dst, src, RELU, bias=zero[:])
 
         def second(c):
             nc.vector.quantize_mx(out=h_codes[c][:].bitcast(FP8X4), scales=h_sc[c][:], in_=h_bf[c][:])
@@ -133,23 +124,24 @@ def tile_list_hboth_m_none_kernel(tc, xT, w1, w2_words, w2_scales, wgt, wgo, off
                                 start=True, stop=True)
 
         def leave(c):
-            if c == 0:
-                nc.vector.tensor_copy(out=y_sb[c], in_=y_ps[c][:])
-            else:
-                nc.scalar.copy(out=y_sb[c], in_=y_ps[c][:])
+            nc.scalar.copy(out=y_sb[c][:], in_=y_ps[c][:])
 
         def place(c0, c1):
             cols = slice(c0 * CH, c1 * CH)
-            nc.vector.tensor_tensor(page[:].indirect(idx2[:, c0 * LC : c1 * LC]), y_tiles[c0][:], wgo_sb[:, cols], MULT)
+            nc.vector.tensor_tensor(page[:].indirect(idx2[:, c0 * LC : c1 * LC]), y_sb[c0][:], wgo_sb[:, cols], MULT)
 
-        for c in range(NCH):
-            pick(PACK - 1, c, c + 1)
-            weave(c, c >= 2)
-            first(c)
-            relu(c, False)
-            second(c)
-            leave(c)
-            if c < 2:
-                place(c, c + 1)
-        place(2, NCH)
+        for step in range(NCH + 4):
+            if step < NCH:
+                pick(PACK - 1, step, step + 1)
+            if 0 <= step - 1 < NCH:
+                weave(step - 1, step - 1 >= 2)
+            if step == 1:
+                nc.vector.quantize_mx(out=w1_codes[:].bitcast(FP8X4), scales=w1_sc[:], in_=w_bf[:])
+            if 0 <= step - 2 < NCH:
+                first(step - 2)
+                relu(step - 2, False)
+            if 0 <= step - 4 < NCH:
+                second(step - 4)
+                leave(step - 4)
+                place(step - 4, step - 3)
         nc.sync.dma_start(out=out, in_=page[:])

@@ -44,21 +44,21 @@ def tile_list_hboth_m_none_kernel(tc, xT, w1, w2_words, w2_scales, wgt, wgo, off
         w1_rows = w1.rearrange("(p j) c -> p j c", j=PACK)
         x_rows = xT.rearrange("(p i) t -> p i t", i=PACK)
 
-        nc.gpsimd.dma_start(out=w2_codes[:].bitcast(I32), in_=w2_words[0].bitcast(I32))
-        nc.gpsimd.memset(w2_sc[:].bitcast(I32), 0)
-        for q in range(4):
-            nc.gpsimd.dma_start(out=w2_sc[32 * q : 32 * q + 4, :].bitcast(I32),
-                                in_=w2_scales[0, 4 * q : 4 * q + 4, :].bitcast(I32))
+        nc.vector.memset(w2_sc[:].bitcast(I32), 0)
         nc.sync.dma_start(out=planes[0][:], in_=x_rows[:, 0, :])
         nc.sync.dma_start(idx[:], offs)
         nc.sync.dma_start(out=wgt_sb[:], in_=wgt)
         nc.sync.dma_start(out=planes[1][:], in_=x_rows[:, 1, :])
         nc.sync.dma_start(out=planes[2][:], in_=x_rows[:, 2, :])
+        nc.sync.dma_start(out=w2_codes[:].bitcast(I32), in_=w2_words[0].bitcast(I32))
         nc.sync.dma_start(out=w_raw[:, 0:2, :], in_=w1_rows[:, 0:2, :])
         nc.sync.dma_start(out=w_raw[:, 2:4, :], in_=w1_rows[:, 2:4, :])
         nc.sync.dma_start(out=planes[3][:], in_=x_rows[:, 3, :])
-        nc.sync.dma_start(idx2[:], offs2)
+        for q in range(4):
+            nc.sync.dma_start(out=w2_sc[32 * q : 32 * q + 4, :].bitcast(I32),
+                              in_=w2_scales[0, 4 * q : 4 * q + 4, :].bitcast(I32))
         nc.sync.dma_start(out=wgo_sb[:], in_=wgo)
+        nc.sync.dma_start(idx2[:], offs2)
         nc.vector.memset(page[:], 0.0)
         zero = sb.tile([P, 1], F32, name="zero")
         nc.scalar.copy(out=zero[:], in_=page[:, 0:1])

@@ -14,15 +14,20 @@ U8 = mybir.dt.uint8
 FP8X4 = mybir.dt.float8_e4m3fn_x4
 FP4X4 = mybir.dt.float4_e2m1fn_x4
 MULT = mybir.AluOpType.mult
-MAX = mybir.AluOpType.max
 RELU = mybir.ActivationFunctionType.Relu
 
 P = 128
 PACK = 4
-CH = 128
-NCH = S // CH
-LC = CH // 16
-W_SCALAR = 72
+GROUP = 16
+QUADRANT = 32
+SCALE_ROWS = 4
+LINE = 4
+CHUNK = 128
+CHUNKS = S // CHUNK
+LIST_COLS = CHUNK // GROUP
+W_ON_SCALAR = 72
+WEAVES_ON_SCALAR = 2
+WEAVE_LAG, FIRST_LAG, SECOND_LAG = 1, 2, 4
 
 
 def tile_list_hboth_m_none_kernel(tc, xT, w1, w2_words, w2_scales, wgt, wgo, offs, offs2, out):
@@ -31,8 +36,8 @@ def tile_list_hboth_m_none_kernel(tc, xT, w1, w2_words, w2_scales, wgt, wgo, off
         sb = ctx.enter_context(tc.tile_pool(name="sb", bufs=1))
         ps = ctx.enter_context(tc.psum_pool(name="ps", bufs=1))
 
-        idx = sb.tile([P, S // 16], U16, name="idx")
-        idx2 = sb.tile([P, S // 16], U16, name="idx2")
+        idx = sb.tile([P, S // GROUP], U16, name="idx")
+        idx2 = sb.tile([P, S // GROUP], U16, name="idx2")
         w_raw = sb.tile([P, PACK, H], F32, name="w_raw")
         planes = [sb.tile([P, T], F32, name="plane%d" % i) for i in range(PACK)]
         wgt_sb = sb.tile([P, S], F32, name="wgt_sb")
@@ -45,20 +50,24 @@ def tile_list_hboth_m_none_kernel(tc, xT, w1, w2_words, w2_scales, wgt, wgo, off
         x_rows = xT.rearrange("(p i) t -> p i t", i=PACK)
 
         nc.vector.memset(w2_sc[:].bitcast(I32), 0)
+
         nc.sync.dma_start(out=planes[0][:], in_=x_rows[:, 0, :])
         nc.sync.dma_start(idx[:], offs)
         nc.sync.dma_start(out=wgt_sb[:], in_=wgt)
         nc.sync.dma_start(out=planes[1][:], in_=x_rows[:, 1, :])
         nc.sync.dma_start(out=planes[2][:], in_=x_rows[:, 2, :])
         nc.sync.dma_start(out=w2_codes[:].bitcast(I32), in_=w2_words[0].bitcast(I32))
-        nc.sync.dma_start(out=w_raw[:, 0:2, :], in_=w1_rows[:, 0:2, :])
-        nc.sync.dma_start(out=w_raw[:, 2:4, :], in_=w1_rows[:, 2:4, :])
-        nc.sync.dma_start(out=planes[3][:], in_=x_rows[:, 3, :])
-        for q in range(4):
-            nc.sync.dma_start(out=w2_sc[32 * q : 32 * q + 4, :].bitcast(I32),
-                              in_=w2_scales[0, 4 * q : 4 * q + 4, :].bitcast(I32))
+        for j in range(0, PACK, 2):
+            nc.sync.dma_start(out=w_raw[:, j : j + 2, :], in_=w1_rows[:, j : j + 2, :])
+        nc.sync.dma_start(out=planes[PACK - 1][:], in_=x_rows[:, PACK - 1, :])
+        for q in range(P // QUADRANT):
+            nc.sync.dma_start(
+                out=w2_sc[QUADRANT * q : QUADRANT * q + SCALE_ROWS, :].bitcast(I32),
+                in_=w2_scales[0, SCALE_ROWS * q : SCALE_ROWS * (q + 1), :].bitcast(I32),
+            )
         nc.sync.dma_start(out=wgo_sb[:], in_=wgo)
         nc.sync.dma_start(idx2[:], offs2)
+
         nc.vector.memset(page[:], 0.0)
         zero = sb.tile([P, 1], F32, name="zero")
         nc.scalar.copy(out=zero[:], in_=page[:, 0:1])
@@ -70,78 +79,78 @@ def tile_list_hboth_m_none_kernel(tc, xT, w1, w2_words, w2_scales, wgt, wgo, off
         picked = sb.tile([P, PACK, S], F32, name="picked")
 
         def pick(i, c0, c1):
-            cols = slice(c0 * CH, c1 * CH)
-            nc.vector.tensor_tensor(picked[:, i, cols], planes[i][:].indirect(idx[:, c0 * LC : c1 * LC]),
-                                    wgt_sb[:, cols], MULT)
+            cols = slice(c0 * CHUNK, c1 * CHUNK)
+            window = planes[i][:].indirect(idx[:, c0 * LIST_COLS : c1 * LIST_COLS])
+            nc.vector.tensor_tensor(picked[:, i, cols], window, wgt_sb[:, cols], MULT)
 
         for i in range(PACK - 1):
-            pick(i, 0, NCH)
+            pick(i, 0, CHUNKS)
         w_src = w_raw[:].rearrange("p j (m t) -> p m j t", t=PACK)
-        nc.scalar.copy(out=w_view[:, 0:W_SCALAR], in_=w_src[:, 0:W_SCALAR])
-        nc.vector.tensor_copy(out=w_view[:, W_SCALAR:P], in_=w_src[:, W_SCALAR:P])
+        nc.scalar.copy(out=w_view[:, 0:W_ON_SCALAR], in_=w_src[:, 0:W_ON_SCALAR])
+        nc.vector.tensor_copy(out=w_view[:, W_ON_SCALAR:P], in_=w_src[:, W_ON_SCALAR:P])
 
         x_bf, x_codes, x_sc, h_ps, h_bf, h_codes, h_sc, y_ps = [], [], [], [], [], [], [], []
-        for c in range(NCH):
-            x_bf.append(sb.tile([P, CH * PACK], BF16, name="x_bf%d" % c, align_bytes=64))
-            x_codes.append(sb.tile([P, CH], U32, name="x_codes%d" % c, align_bytes=64))
-            x_sc.append(sb.tile([P, CH], U8, name="x_sc%d" % c, align_bytes=64))
-            h_bf.append(sb.tile([P, CH * PACK], BF16, name="h_bf%d" % c, align_bytes=64))
-            h_codes.append(sb.tile([P, CH], U32, name="h_codes%d" % c, align_bytes=64))
-            h_sc.append(sb.tile([P, CH], U8, name="h_sc%d" % c, align_bytes=64))
-            h_ps.append(ps.tile([P, PACK, CH], F32, name="h_ps%d" % c))
-            y_ps.append(ps.tile([P, CH], F32, name="y_ps%d" % c))
-        y_sb = [sb.tile([P, CH], F32, name="y_sb%d" % c) for c in range(NCH)]
+        for c in range(CHUNKS):
+            x_bf.append(sb.tile([P, CHUNK * PACK], BF16, name="x_bf%d" % c, align_bytes=64))
+            x_codes.append(sb.tile([P, CHUNK], U32, name="x_codes%d" % c, align_bytes=64))
+            x_sc.append(sb.tile([P, CHUNK], U8, name="x_sc%d" % c, align_bytes=64))
+            h_bf.append(sb.tile([P, CHUNK * PACK], BF16, name="h_bf%d" % c, align_bytes=64))
+            h_codes.append(sb.tile([P, CHUNK], U32, name="h_codes%d" % c, align_bytes=64))
+            h_sc.append(sb.tile([P, CHUNK], U8, name="h_sc%d" % c, align_bytes=64))
+            h_ps.append(ps.tile([P, PACK, CHUNK], F32, name="h_ps%d" % c))
+            y_ps.append(ps.tile([P, CHUNK], F32, name="y_ps%d" % c))
+        y_sb = [sb.tile([P, CHUNK], F32, name="y_sb%d" % c) for c in range(CHUNKS)]
 
-        def weave(c, on_vector):
-            dst = x_bf[c][:].rearrange("p (a s i) -> p a i s", s=4, i=PACK)
-            src = picked[:, :, c * CH : (c + 1) * CH].rearrange("p i (a s) -> p a i s", s=4)
-            if on_vector:
-                nc.vector.tensor_copy(out=dst, in_=src)
-            else:
+        def weave(c):
+            dst = x_bf[c][:].rearrange("p (a s i) -> p a i s", s=LINE, i=PACK)
+            src = picked[:, :, c * CHUNK : (c + 1) * CHUNK].rearrange("p i (a s) -> p a i s", s=LINE)
+            if c < WEAVES_ON_SCALAR:
                 nc.scalar.copy(out=dst, in_=src)
+            else:
+                nc.vector.tensor_copy(out=dst, in_=src)
 
-        def first(c):
+        def first_layer(c):
             nc.vector.quantize_mx(out=x_codes[c][:].bitcast(FP8X4), scales=x_sc[c][:], in_=x_bf[c][:])
             for t in range(PACK):
-                nc.tensor.matmul_mx(out=h_ps[c][:, t, :],
-                                    lhsT=w1_codes[:, t * P : (t + 1) * P].bitcast(FP8X4),
-                                    lhsT_scale=w1_sc[:, t * P : (t + 1) * P],
-                                    rhs=x_codes[c][:].bitcast(FP8X4), rhs_scale=x_sc[c][:],
-                                    start=True, stop=True)
-
-        def relu(c, on_vector):
+                nc.tensor.matmul_mx(
+                    out=h_ps[c][:, t, :],
+                    lhsT=w1_codes[:, t * P : (t + 1) * P].bitcast(FP8X4),
+                    lhsT_scale=w1_sc[:, t * P : (t + 1) * P],
+                    rhs=x_codes[c][:].bitcast(FP8X4),
+                    rhs_scale=x_sc[c][:],
+                    start=True,
+                    stop=True,
+                )
             dst = h_bf[c][:].rearrange("p (s t) -> p s t", t=PACK)
-            src = h_ps[c][:].rearrange("p t s -> p s t")
-            if on_vector:
-                nc.vector.tensor_scalar(dst, src, 0.0, None, MAX)
-            else:
-                nc.scalar.activation(dst, src, RELU, bias=zero[:])
+            nc.scalar.activation(dst, h_ps[c][:].rearrange("p t s -> p s t"), RELU, bias=zero[:])
 
-        def second(c):
+        def second_layer(c):
             nc.vector.quantize_mx(out=h_codes[c][:].bitcast(FP8X4), scales=h_sc[c][:], in_=h_bf[c][:])
-            nc.tensor.matmul_mx(out=y_ps[c][:], lhsT=w2_codes[:].bitcast(FP4X4), lhsT_scale=w2_sc[:],
-                                rhs=h_codes[c][:].bitcast(FP8X4), rhs_scale=h_sc[c][:],
-                                start=True, stop=True)
+            nc.tensor.matmul_mx(
+                out=y_ps[c][:],
+                lhsT=w2_codes[:].bitcast(FP4X4),
+                lhsT_scale=w2_sc[:],
+                rhs=h_codes[c][:].bitcast(FP8X4),
+                rhs_scale=h_sc[c][:],
+                start=True,
+                stop=True,
+            )
+            if c == 0:
+                nc.vector.tensor_copy(out=y_sb[c][:], in_=y_ps[c][:])
+            else:
+                nc.scalar.copy(out=y_sb[c][:], in_=y_ps[c][:])
+            places = page[:].indirect(idx2[:, c * LIST_COLS : (c + 1) * LIST_COLS])
+            nc.vector.tensor_tensor(places, y_sb[c][:], wgo_sb[:, c * CHUNK : (c + 1) * CHUNK], MULT)
 
-        def leave(c):
-            nc.scalar.copy(out=y_sb[c][:], in_=y_ps[c][:])
-
-        def place(c0, c1):
-            cols = slice(c0 * CH, c1 * CH)
-            nc.vector.tensor_tensor(page[:].indirect(idx2[:, c0 * LC : c1 * LC]), y_sb[c0][:], wgo_sb[:, cols], MULT)
-
-        for step in range(NCH + 4):
-            if step < NCH:
+        for step in range(CHUNKS + SECOND_LAG):
+            if step < CHUNKS:
                 pick(PACK - 1, step, step + 1)
-            if 0 <= step - 1 < NCH:
-                weave(step - 1, step - 1 >= 2)
-            if step == 1:
+            if 0 <= step - WEAVE_LAG < CHUNKS:
+                weave(step - WEAVE_LAG)
+            if step == FIRST_LAG - 1:
                 nc.vector.quantize_mx(out=w1_codes[:].bitcast(FP8X4), scales=w1_sc[:], in_=w_bf[:])
-            if 0 <= step - 2 < NCH:
-                first(step - 2)
-                relu(step - 2, False)
-            if 0 <= step - 4 < NCH:
-                second(step - 4)
-                leave(step - 4)
-                place(step - 4, step - 3)
+            if 0 <= step - FIRST_LAG < CHUNKS:
+                first_layer(step - FIRST_LAG)
+            if 0 <= step - SECOND_LAG < CHUNKS:
+                second_layer(step - SECOND_LAG)
         nc.sync.dma_start(out=out, in_=page[:])

from contextlib import ExitStack

import concourse.mybir as mybir

K, H, M, T, S = 512, 512, 128, 1024, 512
FLOPS = 2 * K * H * S + 2 * H * M * S

F32 = mybir.dt.float32
BF16 = mybir.dt.bfloat16
I32 = mybir.dt.int32
U32 = mybir.dt.uint32
U16 = mybir.dt.uint16
U8 = mybir.dt.uint8
FP8X4 = mybir.dt.float8_e4m3fn_x4
FP4X4 = mybir.dt.float4_e2m1fn_x4
MULT = mybir.AluOpType.mult
RELU = mybir.ActivationFunctionType.Relu

P = 128
PACK = 4
GROUP = 16
QUADRANT = 32
SCALE_ROWS = 4
LINE = 4
CHUNK = 128
CHUNKS = S // CHUNK
LIST_COLS = CHUNK // GROUP
W_ON_SCALAR = 72
WEAVES_ON_SCALAR = 2
WEAVE_LAG, FIRST_LAG, SECOND_LAG = 1, 2, 4


def tile_list_hboth_m_none_kernel(tc, xT, w1, w2_words, w2_scales, wgt, wgo, offs, offs2, out):
    nc = tc.nc
    with ExitStack() as ctx:
        sb = ctx.enter_context(tc.tile_pool(name="sb", bufs=1))
        ps = ctx.enter_context(tc.psum_pool(name="ps", bufs=1))

        idx = sb.tile([P, S // GROUP], U16, name="idx")
        idx2 = sb.tile([P, S // GROUP], U16, name="idx2")
        w_raw = sb.tile([P, PACK, H], F32, name="w_raw")
        planes = [sb.tile([P, T], F32, name="plane%d" % i) for i in range(PACK)]
        wgt_sb = sb.tile([P, S], F32, name="wgt_sb")
        wgo_sb = sb.tile([P, S], F32, name="wgo_sb")
        w2_codes = sb.tile([P, 2 * M], U8, name="w2_codes", align_bytes=64)
        w2_sc = sb.tile([P, M], U8, name="w2_sc", align_bytes=64)
        page = sb.tile([P, T], F32, name="page")

        w1_rows = w1.rearrange("(p j) c -> p j c", j=PACK)
        x_rows = xT.rearrange("(p i) t -> p i t", i=PACK)

        nc.vector.memset(w2_sc[:].bitcast(I32), 0)

        nc.sync.dma_start(out=planes[0][:], in_=x_rows[:, 0, :])
        nc.sync.dma_start(idx[:], offs)
        nc.sync.dma_start(out=wgt_sb[:], in_=wgt)
        nc.sync.dma_start(out=planes[1][:], in_=x_rows[:, 1, :])
        nc.sync.dma_start(out=planes[2][:], in_=x_rows[:, 2, :])
        nc.sync.dma_start(out=w2_codes[:].bitcast(I32), in_=w2_words[0].bitcast(I32))
        for j in range(0, PACK, 2):
            nc.sync.dma_start(out=w_raw[:, j : j + 2, :], in_=w1_rows[:, j : j + 2, :])
        nc.sync.dma_start(out=planes[PACK - 1][:], in_=x_rows[:, PACK - 1, :])
        for q in range(P // QUADRANT):
            nc.sync.dma_start(
                out=w2_sc[QUADRANT * q : QUADRANT * q + SCALE_ROWS, :].bitcast(I32),
                in_=w2_scales[0, SCALE_ROWS * q : SCALE_ROWS * (q + 1), :].bitcast(I32),
            )
        nc.sync.dma_start(out=wgo_sb[:], in_=wgo)
        nc.sync.dma_start(idx2[:], offs2)

        nc.vector.memset(page[:], 0.0)
        zero = sb.tile([P, 1], F32, name="zero")
        nc.scalar.copy(out=zero[:], in_=page[:, 0:1])

        w_bf = sb.tile([P, H * PACK], BF16, name="w_bf", align_bytes=64)
        w_view = w_bf[:].rearrange("p (t m j) -> p m j t", t=PACK, j=PACK)
        w1_codes = sb.tile([P, H], U32, name="w1_codes", align_bytes=64)
        w1_sc = sb.tile([P, H], U8, name="w1_sc", align_bytes=64)
        picked = sb.tile([P, PACK, S], F32, name="picked")

        def pick(i, c0, c1):
            cols = slice(c0 * CHUNK, c1 * CHUNK)
            window = planes[i][:].indirect(idx[:, c0 * LIST_COLS : c1 * LIST_COLS])
            nc.vector.tensor_tensor(picked[:, i, cols], window, wgt_sb[:, cols], MULT)

        for i in range(PACK - 1):
            pick(i, 0, CHUNKS)
        w_src = w_raw[:].rearrange("p j (m t) -> p m j t", t=PACK)
        nc.scalar.copy(out=w_view[:, 0:W_ON_SCALAR], in_=w_src[:, 0:W_ON_SCALAR])
        nc.vector.tensor_copy(out=w_view[:, W_ON_SCALAR:P], in_=w_src[:, W_ON_SCALAR:P])

        x_bf, x_codes, x_sc, h_ps, h_bf, h_codes, h_sc, y_ps = [], [], [], [], [], [], [], []
        for c in range(CHUNKS):
            x_bf.append(sb.tile([P, CHUNK * PACK], BF16, name="x_bf%d" % c, align_bytes=64))
            x_codes.append(sb.tile([P, CHUNK], U32, name="x_codes%d" % c, align_bytes=64))
            x_sc.append(sb.tile([P, CHUNK], U8, name="x_sc%d" % c, align_bytes=64))
            h_bf.append(sb.tile([P, CHUNK * PACK], BF16, name="h_bf%d" % c, align_bytes=64))
            h_codes.append(sb.tile([P, CHUNK], U32, name="h_codes%d" % c, align_bytes=64))
            h_sc.append(sb.tile([P, CHUNK], U8, name="h_sc%d" % c, align_bytes=64))
            h_ps.append(ps.tile([P, PACK, CHUNK], F32, name="h_ps%d" % c))
            y_ps.append(ps.tile([P, CHUNK], F32, name="y_ps%d" % c))
        y_sb = [sb.tile([P, CHUNK], F32, name="y_sb%d" % c) for c in range(CHUNKS)]

        def weave(c):
            dst = x_bf[c][:].rearrange("p (a s i) -> p a i s", s=LINE, i=PACK)
            src = picked[:, :, c * CHUNK : (c + 1) * CHUNK].rearrange("p i (a s) -> p a i s", s=LINE)
            if c < WEAVES_ON_SCALAR:
                nc.scalar.copy(out=dst, in_=src)
            else:
                nc.vector.tensor_copy(out=dst, in_=src)

        def first_layer(c):
            nc.vector.quantize_mx(out=x_codes[c][:].bitcast(FP8X4), scales=x_sc[c][:], in_=x_bf[c][:])
            for t in range(PACK):
                nc.tensor.matmul_mx(
                    out=h_ps[c][:, t, :],
                    lhsT=w1_codes[:, t * P : (t + 1) * P].bitcast(FP8X4),
                    lhsT_scale=w1_sc[:, t * P : (t + 1) * P],
                    rhs=x_codes[c][:].bitcast(FP8X4),
                    rhs_scale=x_sc[c][:],
                    start=True,
                    stop=True,
                )
            dst = h_bf[c][:].rearrange("p (s t) -> p s t", t=PACK)
            nc.scalar.activation(dst, h_ps[c][:].rearrange("p t s -> p s t"), RELU, bias=zero[:])

        def second_layer(c):
            nc.vector.quantize_mx(out=h_codes[c][:].bitcast(FP8X4), scales=h_sc[c][:], in_=h_bf[c][:])
            nc.tensor.matmul_mx(
                out=y_ps[c][:],
                lhsT=w2_codes[:].bitcast(FP4X4),
                lhsT_scale=w2_sc[:],
                rhs=h_codes[c][:].bitcast(FP8X4),
                rhs_scale=h_sc[c][:],
                start=True,
                stop=True,
            )
            if c == 0:
                nc.vector.tensor_copy(out=y_sb[c][:], in_=y_ps[c][:])
            else:
                nc.scalar.copy(out=y_sb[c][:], in_=y_ps[c][:])
            places = page[:].indirect(idx2[:, c * LIST_COLS : (c + 1) * LIST_COLS])
            nc.vector.tensor_tensor(places, y_sb[c][:], wgo_sb[:, c * CHUNK : (c + 1) * CHUNK], MULT)

        for step in range(CHUNKS + SECOND_LAG):
            if step < CHUNKS:
                pick(PACK - 1, step, step + 1)
            if 0 <= step - WEAVE_LAG < CHUNKS:
                weave(step - WEAVE_LAG)
            if step == FIRST_LAG - 1:
                nc.vector.quantize_mx(out=w1_codes[:].bitcast(FP8X4), scales=w1_sc[:], in_=w_bf[:])
            if 0 <= step - FIRST_LAG < CHUNKS:
                first_layer(step - FIRST_LAG)
            if 0 <= step - SECOND_LAG < CHUNKS:
                second_layer(step - SECOND_LAG)
        nc.sync.dma_start(out=out, in_=page[:])
